import numpy as np
import ml_dtypes


def mxq(x, axis, fmt="e4m3"):
    dtype, down = {"e4m3": (ml_dtypes.float8_e4m3fn, 7), "e5m2": (ml_dtypes.float8_e5m2, 14)}[fmt]
    v = np.moveaxis(np.asarray(x, np.float32).astype(ml_dtypes.bfloat16).astype(np.float64), axis, -1)
    blocks = v.reshape(v.shape[:-1] + (-1, 32))
    amax = np.abs(blocks).max(-1, keepdims=True)
    byte = np.maximum(np.where(amax > 0, np.frexp(amax)[1] - 1 + 127, 0) - down, 1)
    scale = np.exp2(byte - 127.0)
    codes = (blocks / scale).astype(np.float32).astype(dtype).astype(np.float64)
    return np.moveaxis((codes * scale).reshape(v.shape), -1, axis)


WIDE = False


def mx_kscale(k):
    if not WIDE:
        return np.ones(k)
    levels = np.array([30, -30])
    if k % 512:
        return np.exp2(np.random.permutation(np.resize(levels, k // 32))).repeat(32)
    a = np.empty((k // 512, 16))
    for p in range(k // 512):
        a[p, :8] = np.random.permutation(np.resize(levels, 8))
        for g in range(8):
            far = levels[np.abs(levels - a[p, g]) >= 10]
            a[p, g + 8] = far[np.random.randint(len(far))]
    return np.exp2(a.ravel()).repeat(32)


def f64(x):
    return np.asarray(x).astype(np.float64)


def striped(idx):
    return np.tile(idx.reshape(-1, 16).T, (8, 1)).astype(np.uint16)


def unstriped(offs):
    return offs[:16].T.reshape(-1).astype(np.int64)


E2M1 = np.array([0.0, 0.5, 1.0, 1.5, 2.0, 3.0, 4.0, 6.0, -0.0, -0.5, -1.0, -1.5, -2.0, -3.0, -4.0, -6.0])


def pack_weight(w, fmt):
    k, n = w.shape
    w = f64(np.asarray(w, np.float32).astype(ml_dtypes.bfloat16)).reshape(k // 32, 32, n)
    amax = np.abs(w).max(1)
    if fmt == "e4m3":
        byte = np.frexp(amax)[1] - 1 + 127 - 7
    else:
        mant, ex = np.frexp(amax / 6.0)
        byte = np.where(mant > 0.5, ex, ex - 1) + 127
    byte = np.clip(np.where(amax > 0, byte, 1), 1, 254)
    scaled = (w * np.exp2(127.0 - byte)[:, None, :]).reshape(k, n).astype(np.float32)
    by_word = np.ascontiguousarray(scaled.reshape(k // 512, 128, 4, n).transpose(0, 1, 3, 2))
    if fmt == "e4m3":
        words = by_word.astype(ml_dtypes.float8_e4m3fn).view(np.uint8)
    else:
        c = by_word.astype(ml_dtypes.float4_e2m1fn).view(np.uint8) & 0xF
        words = (c[..., 0::2] | (c[..., 1::2] << 4)).reshape(k // 512, 128, 2 * n)
    return np.ascontiguousarray(words), np.ascontiguousarray(byte.astype(np.uint8).reshape(k // 512, 16, n))


def unpack_weight(words, scales, fmt):
    g, _, n = scales.shape
    words = np.ascontiguousarray(words).reshape(g, 128, n, -1)
    if fmt == "e4m3":
        vals = words.view(ml_dtypes.float8_e4m3fn).astype(np.float64)
    else:
        nib = np.empty((g, 128, n, 4), np.uint8)
        nib[..., 0::2] = words & 0xF
        nib[..., 1::2] = words >> 4
        vals = E2M1[nib]
    vals = vals * np.repeat(np.exp2(scales.astype(np.float64) - 127.0), 8, axis=1)[..., None]
    return vals.transpose(0, 1, 3, 2).reshape(g * 512, n)


K, T, E, C, N = 256, 2048, 2, 512, 1024


def by_expert(wq, xq):
    return np.concatenate([wq[e].T @ xq[:, e * C:(e + 1) * C] for e in range(E)], axis=1)


def setup_inputs():
    n = np.random.standard_normal
    s = mx_kscale(N)[:, None]
    w = [pack_weight(m, "e2m1") for m in n((E + 1, N, K)) / np.sqrt(N) / s[None]]
    return {
        "dyT": (n((N, T)) * s).astype(np.float32),
        "w_words": np.stack([m[0] for m in w]),
        "w_scales": np.stack([m[1] for m in w]),
        "gate": np.tile(np.random.uniform(0.2, 1.0, E * C), (N, 1)).astype(np.float32),
        "offs": striped(np.random.permutation(T)[:E * C]),
    }


def reference(dyT, w_words, w_scales, gate, offs):
    idx = unstriped(offs)
    w = np.stack([unpack_weight(w_words[e], w_scales[e], "e2m1") for e in range(E + 1)])
    gq = mxq(f64(gate) * f64(dyT)[:, idx], 0, "e5m2")
    wq = w
    ds = wq[E].T @ mxq(f64(dyT), 0, "e5m2")
    dx = by_expert(wq, gq)
    ds[:, idx] += dx
    return ds

@@ -1,0 +1,143 @@
+from contextlib import ExitStack
+
+import concourse.mybir as mybir
+from concourse.masks import make_identity
+
+K, T, E, C, N = 256, 2048, 2, 512, 1024
+FLOPS = 2 * N * K * (T + E * C)
+BYTES = 4 * N * T + 4 * K * T + (E + 1) * (N * K // 2 + N * K // 32) + 4 * E * C + 2 * 128 * (E * C // 16)
+
+F32 = mybir.dt.float32
+BF16 = mybir.dt.bfloat16
+I32 = mybir.dt.int32
+U32 = mybir.dt.uint32
+U16 = mybir.dt.uint16
+U8 = mybir.dt.uint8
+E5M2X4 = mybir.dt.float8_e5m2_x4
+E2M1X4 = mybir.dt.float4_e2m1fn_x4
+MULT = mybir.AluOpType.mult
+ADD = mybir.AluOpType.add
+
+P = 128
+PACK = 4
+PASSES = N // (P * PACK)
+KB = K // P
+W = 512
+CHUNKS = T // W
+S = E * C
+
+
+def tile_moe_bds_lin_none_kernel(tc, dyT, w_words, w_scales, gate, offs, out):
+    nc = tc.nc
+    with ExitStack() as ctx:
+        keep = ctx.enter_context(tc.tile_pool(name="keep", bufs=1))
+        psum = ctx.enter_context(tc.psum_pool(name="psum", bufs=1))
+
+        offsets = keep.tile([P, S // 16], U16, name="offsets")
+        nc.sync.dma_start(offsets[:], offs)
+        gate_runs = keep.tile([P, S // P], F32, name="gate_runs")
+        nc.scalar.dma_start(out=gate_runs[:], in_=gate[0:1, :].rearrange("o (p j) -> (o p) j", p=P))
+
+        rows = dyT.rearrange("(a p t) n -> a t p n", a=PASSES, t=PACK)
+        dy = [keep.tile([P, PACK, T], F32, name=f"dy{a}") for a in range(PASSES)]
+        for a in range(PASSES):
+            for t in range(PACK):
+                nc.sync.dma_start(out=dy[a][:, t, :], in_=rows[a, t])
+
+        ww = keep.tile([P, (E + 1) * PASSES, 2 * K], U8, name="ww", align_bytes=64)
+        nc.sync.dma_start(out=ww[:].bitcast(I32), in_=w_words.rearrange("e a p b -> p (e a) b").bitcast(I32))
+        ws = keep.tile([P, (E + 1) * PASSES, K], U8, name="ws", align_bytes=64)
+        nc.vector.memset(ws[:].bitcast(I32), 0)
+        for q in range(4):
+            nc.sync.dma_start(
+                out=ws[32 * q : 32 * q + 4].bitcast(I32),
+                in_=w_scales[:, :, 4 * q : 4 * q + 4, :].rearrange("e a f k -> f (e a) k").bitcast(I32),
+            )
+
+        routed = [keep.tile([P, T], F32, name=f"routed{kb}") for kb in range(KB)]
+        for kb in range(KB):
+            nc.vector.memset(routed[kb][:], 0.0)
+
+        ident = keep.tile([P, P], F32, name="ident")
+        make_identity(nc, ident[:])
+        gates = keep.tile([P, S], F32, name="gates")
+        runs = S // P
+        for h in range(runs // 4):
+            spread = psum.tile([P, 4, P], F32, name="spread", tag=f"bank{h}")
+            for j in range(4):
+                col = 4 * h + j
+                nc.tensor.transpose(spread[:, j, :], gate_runs[:, col : col + 1].to_broadcast([P, P]), ident[:])
+            nc.scalar.copy(
+                out=gates[:].rearrange("p (r j) -> p r j", j=runs)[:, :, 4 * h : 4 * h + 4],
+                in_=spread[:].rearrange("p j r -> p r j"),
+            )
+
+        def round_and_weave(dst, src):
+            nc.scalar.copy(
+                out=dst.rearrange("p (c i) t -> p c t i", i=4),
+                in_=src.rearrange("p t (c i) -> p c t i", i=4),
+            )
+
+        def quantize(woven, name):
+            codes = keep.tile([P, W], U32, name=name + "_codes", align_bytes=64)
+            scales = keep.tile([P, W], U8, name=name + "_scales", align_bytes=64)
+            nc.vector.quantize_mx(
+                out=codes[:].bitcast(E5M2X4), scales=scales[:], in_=woven[:].rearrange("p c t -> p (c t)")
+            )
+            return codes, scales
+
+        def product(acc, e, kb, operands):
+            for a in range(PASSES):
+                codes, scales = operands[a]
+                nc.tensor.matmul_mx(
+                    out=acc[:],
+                    lhsT=ww[:, e * PASSES + a, 2 * P * kb : 2 * P * (kb + 1)].bitcast(E2M1X4),
+                    lhsT_scale=ws[:, e * PASSES + a, P * kb : P * (kb + 1)],
+                    rhs=codes[:].bitcast(E5M2X4),
+                    rhs_scale=scales[:],
+                    start=(a == 0),
+                    stop=(a == PASSES - 1),
+                )
+
+        g_mx = [[None] * PASSES for e in range(E)]
+        dy_mx = [[None] * PASSES for c in range(CHUNKS)]
+
+        def routed_operands(a):
+            g = [keep.tile([P, PACK, C], F32, name=f"g{a}{e}") for e in range(E)]
+            for t in range(PACK):
+                for e in range(E):
+                    nc.vector.tensor_copy(
+                        g[e][:, t, :], dy[a][:, t, :].indirect(offsets[:, e * C // 16 : (e + 1) * C // 16])
+                    )
+                    nc.gpsimd.tensor_tensor(g[e][:, t, :], g[e][:, t, :], gates[:, e * C : (e + 1) * C], MULT)
+            for e in range(E):
+                woven = keep.tile([P, C, PACK], BF16, name=f"gw{a}{e}", align_bytes=64)
+                round_and_weave(woven[:], g[e][:])
+                g_mx[e][a] = quantize(woven, f"g{a}{e}")
+
+        def shared_operand(a, c):
+            woven = keep.tile([P, W, PACK], BF16, name="dw", tag=f"dw{c}", align_bytes=64)
+            round_and_weave(woven[:], dy[a][:, :, c * W : (c + 1) * W])
+            dy_mx[c][a] = quantize(woven, f"dy{a}{c}")
+
+        routed_operands(0)
+        routed_operands(1)
+        for e in range(E):
+            for kb in range(KB):
+                acc = psum.tile([P, C], F32, name="acc", tag=f"bank{e * KB + kb}")
+                product(acc, e, kb, g_mx[e])
+                dx = keep.tile([P, C], F32, name=f"dx{e}{kb}")
+                nc.scalar.copy(out=dx[:], in_=acc[:])
+                nc.vector.tensor_copy(routed[kb][:].indirect(offsets[:, e * C // 16 : (e + 1) * C // 16]), dx[:])
+
+        for a in range(PASSES):
+            for c in range(CHUNKS):
+                shared_operand(a, c)
+
+        for kb in range(KB):
+            for c in range(CHUNKS):
+                cols = slice(c * W, (c + 1) * W)
+                acc = psum.tile([P, W], F32, name="ds", tag=f"bank{(4 * (1 - kb)) + c}")
+                product(acc, E, kb, dy_mx[c])
+                nc.vector.tensor_tensor(routed[kb][:, cols], acc[:], routed[kb][:, cols], ADD)
+                nc.sync.dma_start(out=out[kb * P : (kb + 1) * P, cols], in_=routed[kb][:, cols])

@@ -25,6 +25,10 @@ KB = K // P
 W = 512
 CHUNKS = T // W
 S = E * C
+EARLY = 2
+PIECE = 256
+BLOCKS = S // P
+COPY = mybir.ActivationFunctionType.Copy
 
 
 def tile_moe_bds_lin_none_kernel(tc, dyT, w_words, w_scales, gate, offs, out):
@@ -35,19 +39,42 @@ def tile_moe_bds_lin_none_kernel(tc, dyT, w_words, w_scales, gate, offs, out):
 
         offsets = keep.tile([P, S // 16], U16, name="offsets")
         nc.sync.dma_start(offsets[:], offs)
-        gate_runs = keep.tile([P, S // P], F32, name="gate_runs")
+        gate_runs = keep.tile([P, BLOCKS], F32, name="gate_runs")
         nc.scalar.dma_start(out=gate_runs[:], in_=gate[0:1, :].rearrange("o (p j) -> (o p) j", p=P))
+
+        ident = keep.tile([P, P], F32, name="ident")
+        make_identity(nc, ident[:])
+        gate_row = keep.tile([P, S], F32, name="gate_row")
+        for h in range(2):
+            spread = psum.tile([P, 4, P], F32, name="spread", tag=f"bank{4 + h}")
+            for j in range(4):
+                col = 4 * h + j
+                nc.tensor.transpose(spread[:, j, :], gate_runs[:, col : col + 1].to_broadcast([P, P]), ident[:])
+            nc.scalar.copy(
+                out=gate_row[:].rearrange("p (r j) -> p r j", j=BLOCKS)[:, :, 4 * h : 4 * h + 4],
+                in_=spread[:].rearrange("p j r -> p r j"),
+            )
+        gates = keep.tile([P, BLOCKS], F32, name="gates")
+        for h in range(2):
+            columns = psum.tile([P, 4, P], F32, name="columns", tag=f"bank{6 + h}")
+            for j in range(4):
+                block = 4 * h + j
+                nc.tensor.transpose(columns[:, j, :], gate_row[:, block * P : (block + 1) * P], ident[:])
+            nc.scalar.copy(out=gates[:, 4 * h : 4 * h + 4], in_=columns[:, :, 0])
 
         rows = dyT.rearrange("(a p t) n -> a t p n", a=PASSES, t=PACK)
         dy = [keep.tile([P, PACK, T], F32, name=f"dy{a}") for a in range(PASSES)]
         for a in range(PASSES):
-            for t in range(PACK):
+            for t in range(PACK - 1):
                 nc.sync.dma_start(out=dy[a][:, t, :], in_=rows[a, t])
+            for h in range(2):
+                half = slice(h * T // 2, (h + 1) * T // 2)
+                nc.sync.dma_start(out=dy[a][:, PACK - 1, half], in_=rows[a, PACK - 1][:, half])
 
         ww = keep.tile([P, (E + 1) * PASSES, 2 * K], U8, name="ww", align_bytes=64)
         nc.sync.dma_start(out=ww[:].bitcast(I32), in_=w_words.rearrange("e a p b -> p (e a) b").bitcast(I32))
         ws = keep.tile([P, (E + 1) * PASSES, K], U8, name="ws", align_bytes=64)
-        nc.vector.memset(ws[:].bitcast(I32), 0)
+        nc.gpsimd.memset(ws[:].bitcast(I32), 0)
         for q in range(4):
             nc.sync.dma_start(
                 out=ws[32 * q : 32 * q + 4].bitcast(I32),
@@ -56,21 +83,7 @@ def tile_moe_bds_lin_none_kernel(tc, dyT, w_words, w_scales, gate, offs, out):
 
         routed = [keep.tile([P, T], F32, name=f"routed{kb}") for kb in range(KB)]
         for kb in range(KB):
-            nc.vector.memset(routed[kb][:], 0.0)
-
-        ident = keep.tile([P, P], F32, name="ident")
-        make_identity(nc, ident[:])
-        gates = keep.tile([P, S], F32, name="gates")
-        runs = S // P
-        for h in range(runs // 4):
-            spread = psum.tile([P, 4, P], F32, name="spread", tag=f"bank{h}")
-            for j in range(4):
-                col = 4 * h + j
-                nc.tensor.transpose(spread[:, j, :], gate_runs[:, col : col + 1].to_broadcast([P, P]), ident[:])
-            nc.scalar.copy(
-                out=gates[:].rearrange("p (r j) -> p r j", j=runs)[:, :, 4 * h : 4 * h + 4],
-                in_=spread[:].rearrange("p j r -> p r j"),
-            )
+            nc.gpsimd.memset(routed[kb][:], 0.0)
 
         def round_and_weave(dst, src):
             nc.scalar.copy(
@@ -79,12 +92,13 @@ def tile_moe_bds_lin_none_kernel(tc, dyT, w_words, w_scales, gate, offs, out):
             )
 
         def quantize(woven, name):
-            codes = keep.tile([P, W], U32, name=name + "_codes", align_bytes=64)
-            scales = keep.tile([P, W], U8, name=name + "_scales", align_bytes=64)
+            width = woven.shape[1]
+            codes = keep.tile([P, width], U32, name=name + "_codes", align_bytes=64)
+            scales = keep.tile([P, width], U8, name=name + "_scales", align_bytes=64)
             nc.vector.quantize_mx(
-                out=codes[:].bitcast(E5M2X4), scales=scales[:], in_=woven[:].rearrange("p c t -> p (c t)")
+                out=codes[:].bitcast(E5M2X4), scales=scales[:], in_=woven.rearrange("p c t -> p (c t)")
             )
-            return codes, scales
+            return [(codes[:, w : w + W], scales[:, w : w + W]) for w in range(0, width, W)]
 
         def product(acc, e, kb, operands):
             for a in range(PASSES):
@@ -93,51 +107,97 @@ def tile_moe_bds_lin_none_kernel(tc, dyT, w_words, w_scales, gate, offs, out):
                     out=acc[:],
                     lhsT=ww[:, e * PASSES + a, 2 * P * kb : 2 * P * (kb + 1)].bitcast(E2M1X4),
                     lhsT_scale=ws[:, e * PASSES + a, P * kb : P * (kb + 1)],
-                    rhs=codes[:].bitcast(E5M2X4),
-                    rhs_scale=scales[:],
+                    rhs=codes.bitcast(E5M2X4),
+                    rhs_scale=scales,
                     start=(a == 0),
                     stop=(a == PASSES - 1),
                 )
 
-        g_mx = [[None] * PASSES for e in range(E)]
-        dy_mx = [[None] * PASSES for c in range(CHUNKS)]
+        def expert_offsets(e):
+            return offsets[:, e * C // 16 : (e + 1) * C // 16]
 
-        def routed_operands(a):
-            g = [keep.tile([P, PACK, C], F32, name=f"g{a}{e}") for e in range(E)]
-            for t in range(PACK):
-                for e in range(E):
-                    nc.vector.tensor_copy(
-                        g[e][:, t, :], dy[a][:, t, :].indirect(offsets[:, e * C // 16 : (e + 1) * C // 16])
-                    )
-                    nc.gpsimd.tensor_tensor(g[e][:, t, :], g[e][:, t, :], gates[:, e * C : (e + 1) * C], MULT)
+        def gather(a):
+            picked = keep.tile([P, PACK, S], F32, name=f"picked{a}", align_bytes=64)
+            for t in range(PACK - 1):
+                nc.vector.tensor_copy(picked[:, t, :], dy[a][:, t, :].indirect(offsets[:]))
             for e in range(E):
-                woven = keep.tile([P, C, PACK], BF16, name=f"gw{a}{e}", align_bytes=64)
-                round_and_weave(woven[:], g[e][:])
-                g_mx[e][a] = quantize(woven, f"g{a}{e}")
+                nc.vector.tensor_copy(
+                    picked[:, PACK - 1, e * C : (e + 1) * C], dy[a][:, PACK - 1, :].indirect(expert_offsets(e))
+                )
+            return picked
 
-        def shared_operand(a, c):
-            woven = keep.tile([P, W, PACK], BF16, name="dw", tag=f"dw{c}", align_bytes=64)
-            round_and_weave(woven[:], dy[a][:, :, c * W : (c + 1) * W])
-            dy_mx[c][a] = quantize(woven, f"dy{a}{c}")
+        def gate_and_weave(woven, picked, e):
+            woven_words = woven.rearrange("p c t -> p (c t)").bitcast(F32)
+            for h in range(2):
+                back = psum.tile([P, 2, 2, P], F32, name="back", tag=f"bank{4 + h}")
+                for i in range(2):
+                    block = e * (C // P) + 2 * h + i
+                    turned = psum.tile([P, PACK, P], F32, name="turned", tag=f"bank{block % 4}")
+                    for t in reversed(range(PACK)):
+                        nc.tensor.transpose(turned[:, t, :], picked[:, t, block * P : (block + 1) * P], ident[:])
+                    pairs = keep.tile([P, 2, P, 2], BF16, name="pairs", tag="pairs", bufs=4)
+                    nc.scalar.activation(
+                        out=pairs[:],
+                        in_=turned[:].rearrange("s (u j) p -> s u p j", j=2),
+                        func=COPY,
+                        scale=gates[:, block : block + 1],
+                    )
+                    pair_words = pairs[:].rearrange("s u p j -> s (u p j)").bitcast(F32)
+                    for u in range(2):
+                        nc.tensor.transpose(back[:, i, u, :], pair_words[:, u * P : (u + 1) * P], ident[:])
+                nc.scalar.copy(
+                    out=woven_words[:, h * C : (h + 1) * C].rearrange("p (i s u) -> p i s u", i=2, u=2),
+                    in_=back[:].rearrange("p i u s -> p i s u"),
+                )
 
-        routed_operands(0)
-        routed_operands(1)
+        picked = gather(0)
+        g_first = keep.tile([P, S, PACK], BF16, name="g_first", align_bytes=64)
         for e in range(E):
+            gate_and_weave(g_first[:, e * C : (e + 1) * C, :], picked, e)
+        picked = gather(1)
+        g_mx = [[operand] for operand in quantize(g_first[:], "g_first")]
+
+        def routed_product(bank, e, kb):
+            acc = psum.tile([P, C], F32, name="acc", tag=f"bank{bank}")
+            product(acc, e, kb, g_mx[e])
+            dx = keep.tile([P, C], F32, name=f"dx{e}{kb}")
+            nc.scalar.copy(out=dx[:], in_=acc[:])
+            nc.vector.tensor_copy(routed[kb][:].indirect(expert_offsets(e)), dx[:])
+
+        for e in range(E):
+            slots = slice(e * C, (e + 1) * C)
+            woven = keep.tile([P, C, PACK], BF16, name=f"g_second{e}", align_bytes=64)
+            nc.vector.tensor_tensor(
+                woven[:].rearrange("p (c i) t -> p c t i", i=2),
+                picked[:, :, slots].rearrange("p t (c i) -> p c t i", i=2),
+                gate_row[:, slots].rearrange("p (c i) -> p c i", i=2).unsqueeze(2).to_broadcast([P, C // 2, PACK, 2]),
+                MULT,
+            )
+            g_mx[e].extend(quantize(woven[:], f"g_second{e}"))
             for kb in range(KB):
-                acc = psum.tile([P, C], F32, name="acc", tag=f"bank{e * KB + kb}")
-                product(acc, e, kb, g_mx[e])
-                dx = keep.tile([P, C], F32, name=f"dx{e}{kb}")
-                nc.scalar.copy(out=dx[:], in_=acc[:])
-                nc.vector.tensor_copy(routed[kb][:].indirect(offsets[:, e * C // 16 : (e + 1) * C // 16]), dx[:])
+                routed_product(KB * e + kb, e, kb)
 
-        for a in range(PASSES):
-            for c in range(CHUNKS):
-                shared_operand(a, c)
+        def shared_operands(woven, a, first):
+            for j in range(0, woven.shape[1], PIECE):
+                round_and_weave(woven[:, j : j + PIECE, :], dy[a][:, :, first * W + j : first * W + j + PIECE])
+            for i, operand in enumerate(quantize(woven, f"dy{a}{first}")):
+                dy_mx[first + i].append(operand)
 
-        for kb in range(KB):
-            for c in range(CHUNKS):
+        dy_mx = [[] for c in range(CHUNKS)]
+        early = keep.tile([P, EARLY * W, PACK], BF16, name="early", align_bytes=64)
+        shared_operands(early[:], 0, 0)
+        late = keep.tile([P, (2 * CHUNKS - EARLY) * W * PACK], BF16, name="late", tag="picked0", align_bytes=64)
+        rooms = [late[:, c * W * PACK : (c + 1) * W * PACK] for c in range(CHUNKS)]
+        rest = late[:, T * PACK :].rearrange("p (c t) -> p c t", t=PACK)
+        shared_operands(rest, 0, 2)
+        for c in range(CHUNKS):
+            shared_operands(rooms[c].rearrange("p (c t) -> p c t", t=PACK), 1, c)
+
+        for c in range(CHUNKS):
+            result = rooms[(c + 1) % CHUNKS].bitcast(F32)
+            for kb in range(KB):
                 cols = slice(c * W, (c + 1) * W)
-                acc = psum.tile([P, W], F32, name="ds", tag=f"bank{(4 * (1 - kb)) + c}")
+                acc = psum.tile([P, W], F32, name="ds", tag=f"bank{KB * c + kb}")
                 product(acc, E, kb, dy_mx[c])
-                nc.vector.tensor_tensor(routed[kb][:, cols], acc[:], routed[kb][:, cols], ADD)
-                nc.sync.dma_start(out=out[kb * P : (kb + 1) * P, cols], in_=routed[kb][:, cols])
+                nc.vector.tensor_tensor(result[:, kb * W : (kb + 1) * W], acc[:], routed[kb][:, cols], ADD)
+                nc.sync.dma_start(out=out[kb * P : (kb + 1) * P, cols], in_=result[:, kb * W : (kb + 1) * W])

@@ -17,6 +17,7 @@ E5M2X4 = mybir.dt.float8_e5m2_x4
 E2M1X4 = mybir.dt.float4_e2m1fn_x4
 MULT = mybir.AluOpType.mult
 ADD = mybir.AluOpType.add
+COPY = mybir.ActivationFunctionType.Copy
 
 P = 128
 PACK = 4
@@ -25,10 +26,12 @@ KB = K // P
 W = 512
 CHUNKS = T // W
 S = E * C
+BLOCKS = S // P
+PER_BANK = W // P
+PER_COLUMN = 16
+LINE = 4
 EARLY = 2
 PIECE = 256
-BLOCKS = S // P
-COPY = mybir.ActivationFunctionType.Copy
 
 
 def tile_moe_bds_lin_none_kernel(tc, dyT, w_words, w_scales, gate, offs, out):
@@ -37,39 +40,42 @@ def tile_moe_bds_lin_none_kernel(tc, dyT, w_words, w_scales, gate, offs, out):
         keep = ctx.enter_context(tc.tile_pool(name="keep", bufs=1))
         psum = ctx.enter_context(tc.psum_pool(name="psum", bufs=1))
 
-        offsets = keep.tile([P, S // 16], U16, name="offsets")
+        offsets = keep.tile([P, S // PER_COLUMN], U16, name="offsets")
         nc.sync.dma_start(offsets[:], offs)
+
         gate_runs = keep.tile([P, BLOCKS], F32, name="gate_runs")
         nc.scalar.dma_start(out=gate_runs[:], in_=gate[0:1, :].rearrange("o (p j) -> (o p) j", p=P))
-
         ident = keep.tile([P, P], F32, name="ident")
         make_identity(nc, ident[:])
+
         gate_row = keep.tile([P, S], F32, name="gate_row")
-        for h in range(2):
-            spread = psum.tile([P, 4, P], F32, name="spread", tag=f"bank{4 + h}")
-            for j in range(4):
-                col = 4 * h + j
+        for h in range(BLOCKS // PER_BANK):
+            spread = psum.tile([P, PER_BANK, P], F32, name="spread", tag=f"bank{4 + h}")
+            for j in range(PER_BANK):
+                col = PER_BANK * h + j
                 nc.tensor.transpose(spread[:, j, :], gate_runs[:, col : col + 1].to_broadcast([P, P]), ident[:])
             nc.scalar.copy(
-                out=gate_row[:].rearrange("p (r j) -> p r j", j=BLOCKS)[:, :, 4 * h : 4 * h + 4],
+                out=gate_row[:].rearrange("p (r j) -> p r j", j=BLOCKS)[:, :, PER_BANK * h : PER_BANK * (h + 1)],
                 in_=spread[:].rearrange("p j r -> p r j"),
             )
-        gates = keep.tile([P, BLOCKS], F32, name="gates")
-        for h in range(2):
-            columns = psum.tile([P, 4, P], F32, name="columns", tag=f"bank{6 + h}")
-            for j in range(4):
-                block = 4 * h + j
+        gate_cols = keep.tile([P, BLOCKS], F32, name="gates")
+        for h in range(BLOCKS // PER_BANK):
+            columns = psum.tile([P, PER_BANK, P], F32, name="columns", tag=f"bank{6 + h}")
+            for j in range(PER_BANK):
+                block = PER_BANK * h + j
                 nc.tensor.transpose(columns[:, j, :], gate_row[:, block * P : (block + 1) * P], ident[:])
-            nc.scalar.copy(out=gates[:, 4 * h : 4 * h + 4], in_=columns[:, :, 0])
+            nc.scalar.copy(out=gate_cols[:, PER_BANK * h : PER_BANK * (h + 1)], in_=columns[:, :, 0])
 
         rows = dyT.rearrange("(a p t) n -> a t p n", a=PASSES, t=PACK)
-        dy = [keep.tile([P, PACK, T], F32, name=f"dy{a}") for a in range(PASSES)]
-        for a in range(PASSES):
-            for t in range(PACK - 1):
-                nc.sync.dma_start(out=dy[a][:, t, :], in_=rows[a, t])
-            for h in range(2):
-                half = slice(h * T // 2, (h + 1) * T // 2)
-                nc.sync.dma_start(out=dy[a][:, PACK - 1, half], in_=rows[a, PACK - 1][:, half])
+        dy = [keep.tile([P, PACK, T], F32, name="dy0"), keep.tile([P, PACK, T], F32, name="dy1", tag="gate_runs")]
+        for t in range(PACK - 1):
+            nc.sync.dma_start(out=dy[0][:, t, :], in_=rows[0, t])
+        for h in range(2):
+            half = slice(h * T // 2, (h + 1) * T // 2)
+            nc.sync.dma_start(out=dy[0][:, PACK - 1, half], in_=rows[0, PACK - 1][:, half])
+        planes = [keep.tile([P, T], F32, name=f"plane{t}") for t in range(PACK)]
+        for t in range(PACK):
+            nc.sync.dma_start(out=planes[t][:], in_=rows[1, t])
 
         ww = keep.tile([P, (E + 1) * PASSES, 2 * K], U8, name="ww", align_bytes=64)
         nc.sync.dma_start(out=ww[:].bitcast(I32), in_=w_words.rearrange("e a p b -> p (e a) b").bitcast(I32))
@@ -81,14 +87,18 @@ def tile_moe_bds_lin_none_kernel(tc, dyT, w_words, w_scales, gate, offs, out):
                 in_=w_scales[:, :, 4 * q : 4 * q + 4, :].rearrange("e a f k -> f (e a) k").bitcast(I32),
             )
 
-        routed = [keep.tile([P, T], F32, name=f"routed{kb}") for kb in range(KB)]
-        for kb in range(KB):
-            nc.gpsimd.memset(routed[kb][:], 0.0)
+        for c in range(CHUNKS):
+            cols = slice(c * W, (c + 1) * W)
+            nc.sync.dma_start(out=dy[1][:, :, cols], in_=rows[1].rearrange("t p n -> p t n")[:, :, cols])
 
-        def round_and_weave(dst, src):
-            nc.scalar.copy(
-                out=dst.rearrange("p (c i) t -> p c t i", i=4),
-                in_=src.rearrange("p t (c i) -> p c t i", i=4),
+        routed = [keep.tile([P, T], F32, name=f"routed{kb}") for kb in range(KB)]
+        nc.vector.memset(routed[0][:], 0.0)
+        nc.gpsimd.memset(routed[1][:], 0.0)
+
+        def round_and_weave(dst, src, copy=nc.scalar.copy):
+            copy(
+                out=dst.rearrange("p (c i) t -> p c t i", i=LINE),
+                in_=src.rearrange("p t (c i) -> p c t i", i=LINE),
             )
 
         def quantize(woven, name):
@@ -114,20 +124,19 @@ def tile_moe_bds_lin_none_kernel(tc, dyT, w_words, w_scales, gate, offs, out):
                 )
 
         def expert_offsets(e):
-            return offsets[:, e * C // 16 : (e + 1) * C // 16]
+            return offsets[:, e * C // PER_COLUMN : (e + 1) * C // PER_COLUMN]
 
-        def gather(a):
-            picked = keep.tile([P, PACK, S], F32, name=f"picked{a}", align_bytes=64)
-            for t in range(PACK - 1):
-                nc.vector.tensor_copy(picked[:, t, :], dy[a][:, t, :].indirect(offsets[:]))
-            for e in range(E):
-                nc.vector.tensor_copy(
-                    picked[:, PACK - 1, e * C : (e + 1) * C], dy[a][:, PACK - 1, :].indirect(expert_offsets(e))
-                )
-            return picked
+        picked = keep.tile([P, PACK, S], F32, name="picked0", align_bytes=64)
+        for t in range(PACK - 1):
+            nc.vector.tensor_copy(picked[:, t, :], dy[0][:, t, :].indirect(offsets[:]))
+        for e in range(E):
+            nc.vector.tensor_copy(
+                picked[:, PACK - 1, e * C : (e + 1) * C], dy[0][:, PACK - 1, :].indirect(expert_offsets(e))
+            )
 
-        def gate_and_weave(woven, picked, e):
-            woven_words = woven.rearrange("p c t -> p (c t)").bitcast(F32)
+        g_first = keep.tile([P, S, PACK], BF16, name="g_first", align_bytes=64)
+        for e in range(E):
+            woven_words = g_first[:, e * C : (e + 1) * C, :].rearrange("p c t -> p (c t)").bitcast(F32)
             for h in range(2):
                 back = psum.tile([P, 2, 2, P], F32, name="back", tag=f"bank{4 + h}")
                 for i in range(2):
@@ -135,12 +144,12 @@ def tile_moe_bds_lin_none_kernel(tc, dyT, w_words, w_scales, gate, offs, out):
                     turned = psum.tile([P, PACK, P], F32, name="turned", tag=f"bank{block % 4}")
                     for t in reversed(range(PACK)):
                         nc.tensor.transpose(turned[:, t, :], picked[:, t, block * P : (block + 1) * P], ident[:])
-                    pairs = keep.tile([P, 2, P, 2], BF16, name="pairs", tag="pairs", bufs=4)
+                    pairs = keep.tile([P, 2, P, 2], BF16, name="pairs", tag=f"pairs{block % 4}", align_bytes=64)
                     nc.scalar.activation(
                         out=pairs[:],
                         in_=turned[:].rearrange("s (u j) p -> s u p j", j=2),
                         func=COPY,
-                        scale=gates[:, block : block + 1],
+                        scale=gate_cols[:, block : block + 1],
                     )
                     pair_words = pairs[:].rearrange("s u p j -> s (u p j)").bitcast(F32)
                     for u in range(2):
@@ -150,51 +159,47 @@ def tile_moe_bds_lin_none_kernel(tc, dyT, w_words, w_scales, gate, offs, out):
                     in_=back[:].rearrange("p i u s -> p i s u"),
                 )
 
-        picked = gather(0)
-        g_first = keep.tile([P, S, PACK], BF16, name="g_first", align_bytes=64)
-        for e in range(E):
-            gate_and_weave(g_first[:, e * C : (e + 1) * C, :], picked, e)
-        picked = gather(1)
-        g_mx = [[operand] for operand in quantize(g_first[:], "g_first")]
-
-        def routed_product(bank, e, kb):
-            acc = psum.tile([P, C], F32, name="acc", tag=f"bank{bank}")
-            product(acc, e, kb, g_mx[e])
-            dx = keep.tile([P, C], F32, name=f"dx{e}{kb}")
-            nc.scalar.copy(out=dx[:], in_=acc[:])
-            nc.vector.tensor_copy(routed[kb][:].indirect(expert_offsets(e)), dx[:])
-
+        gated = keep.tile([P, PACK, S], F32, name="gated", align_bytes=64)
+        for t in range(PACK - 1):
+            nc.vector.tensor_tensor(gated[:, t, :], planes[t][:].indirect(offsets[:]), gate_row[:], MULT)
         for e in range(E):
             slots = slice(e * C, (e + 1) * C)
-            woven = keep.tile([P, C, PACK], BF16, name=f"g_second{e}", align_bytes=64)
             nc.vector.tensor_tensor(
-                woven[:].rearrange("p (c i) t -> p c t i", i=2),
-                picked[:, :, slots].rearrange("p t (c i) -> p c t i", i=2),
-                gate_row[:, slots].rearrange("p (c i) -> p c i", i=2).unsqueeze(2).to_broadcast([P, C // 2, PACK, 2]),
-                MULT,
+                gated[:, PACK - 1, slots], planes[PACK - 1][:].indirect(expert_offsets(e)), gate_row[:, slots], MULT
             )
-            g_mx[e].extend(quantize(woven[:], f"g_second{e}"))
+        g_mx = [[operand] for operand in quantize(g_first[:], "g_first")]
+
+        for e, copy in enumerate((nc.scalar.copy, nc.vector.tensor_copy)):
+            g_second = keep.tile([P, C, PACK], BF16, name="g_second", tag="pairs3", align_bytes=64)
+            round_and_weave(g_second[:], gated[:, :, e * C : (e + 1) * C], copy)
+            g_mx[e].extend(quantize(g_second[:], f"g_second{e}"))
             for kb in range(KB):
-                routed_product(KB * e + kb, e, kb)
+                acc = psum.tile([P, C], F32, name="acc", tag=f"bank{kb}")
+                product(acc, e, kb, g_mx[e])
+                dx = keep.tile([P, C], F32, name=f"dx{e}{kb}")
+                nc.scalar.copy(out=dx[:], in_=acc[:])
+                nc.vector.tensor_copy(routed[kb][:].indirect(expert_offsets(e)), dx[:])
+
+        dy_mx = [[] for c in range(CHUNKS)]
 
         def shared_operands(woven, a, first):
             for j in range(0, woven.shape[1], PIECE):
                 round_and_weave(woven[:, j : j + PIECE, :], dy[a][:, :, first * W + j : first * W + j + PIECE])
             for i, operand in enumerate(quantize(woven, f"dy{a}{first}")):
-                dy_mx[first + i].append(operand)
+                dy_mx[first + i].insert(a, operand)
 
-        dy_mx = [[] for c in range(CHUNKS)]
         early = keep.tile([P, EARLY * W, PACK], BF16, name="early", align_bytes=64)
         shared_operands(early[:], 0, 0)
-        late = keep.tile([P, (2 * CHUNKS - EARLY) * W * PACK], BF16, name="late", tag="picked0", align_bytes=64)
-        rooms = [late[:, c * W * PACK : (c + 1) * W * PACK] for c in range(CHUNKS)]
-        rest = late[:, T * PACK :].rearrange("p (c t) -> p c t", t=PACK)
-        shared_operands(rest, 0, 2)
-        for c in range(CHUNKS):
-            shared_operands(rooms[c].rearrange("p (c t) -> p c t", t=PACK), 1, c)
+        late = keep.tile([P, (PASSES * CHUNKS - EARLY) * W * PACK], BF16, name="late", tag="picked0", align_bytes=64)
+
+        def rooms(first, count):
+            return late[:, first * W * PACK : (first + count) * W * PACK]
+
+        for a, first, count, room in ((1, 0, 1, 0), (0, EARLY, 2, CHUNKS), (1, 1, 1, 1), (1, 2, 2, 2)):
+            shared_operands(rooms(room, count).rearrange("p (c t) -> p c t", t=PACK), a, first)
 
         for c in range(CHUNKS):
-            result = rooms[(c + 1) % CHUNKS].bitcast(F32)
+            result = rooms((c + 1) % CHUNKS, 1).bitcast(F32)
             for kb in range(KB):
                 cols = slice(c * W, (c + 1) * W)
                 acc = psum.tile([P, W], F32, name="ds", tag=f"bank{KB * c + kb}")

from contextlib import ExitStack

import concourse.mybir as mybir
from concourse.masks import make_identity

K, T, E, C, N = 256, 2048, 2, 512, 1024
FLOPS = 2 * N * K * (T + E * C)
BYTES = 4 * N * T + 4 * K * T + (E + 1) * (N * K // 2 + N * K // 32) + 4 * E * C + 2 * 128 * (E * C // 16)

F32 = mybir.dt.float32
BF16 = mybir.dt.bfloat16
I32 = mybir.dt.int32
U32 = mybir.dt.uint32
U16 = mybir.dt.uint16
U8 = mybir.dt.uint8
E5M2X4 = mybir.dt.float8_e5m2_x4
E2M1X4 = mybir.dt.float4_e2m1fn_x4
MULT = mybir.AluOpType.mult
ADD = mybir.AluOpType.add
COPY = mybir.ActivationFunctionType.Copy

P = 128
PACK = 4
PASSES = N // (P * PACK)
KB = K // P
W = 512
CHUNKS = T // W
S = E * C
BLOCKS = S // P
PER_BANK = W // P
PER_COLUMN = 16
LINE = 4
EARLY = 2
PIECE = 256


def tile_moe_bds_lin_none_kernel(tc, dyT, w_words, w_scales, gate, offs, out):
    nc = tc.nc
    with ExitStack() as ctx:
        keep = ctx.enter_context(tc.tile_pool(name="keep", bufs=1))
        psum = ctx.enter_context(tc.psum_pool(name="psum", bufs=1))

        offsets = keep.tile([P, S // PER_COLUMN], U16, name="offsets")
        nc.sync.dma_start(offsets[:], offs)

        gate_runs = keep.tile([P, BLOCKS], F32, name="gate_runs")
        nc.scalar.dma_start(out=gate_runs[:], in_=gate[0:1, :].rearrange("o (p j) -> (o p) j", p=P))
        ident = keep.tile([P, P], F32, name="ident")
        make_identity(nc, ident[:])

        gate_row = keep.tile([P, S], F32, name="gate_row")
        for h in range(BLOCKS // PER_BANK):
            spread = psum.tile([P, PER_BANK, P], F32, name="spread", tag=f"bank{4 + h}")
            for j in range(PER_BANK):
                col = PER_BANK * h + j
                nc.tensor.transpose(spread[:, j, :], gate_runs[:, col : col + 1].to_broadcast([P, P]), ident[:])
            nc.scalar.copy(
                out=gate_row[:].rearrange("p (r j) -> p r j", j=BLOCKS)[:, :, PER_BANK * h : PER_BANK * (h + 1)],
                in_=spread[:].rearrange("p j r -> p r j"),
            )
        gate_cols = keep.tile([P, BLOCKS], F32, name="gates")
        for h in range(BLOCKS // PER_BANK):
            columns = psum.tile([P, PER_BANK, P], F32, name="columns", tag=f"bank{6 + h}")
            for j in range(PER_BANK):
                block = PER_BANK * h + j
                nc.tensor.transpose(columns[:, j, :], gate_row[:, block * P : (block + 1) * P], ident[:])
            nc.scalar.copy(out=gate_cols[:, PER_BANK * h : PER_BANK * (h + 1)], in_=columns[:, :, 0])

        rows = dyT.rearrange("(a p t) n -> a t p n", a=PASSES, t=PACK)
        dy = [keep.tile([P, PACK, T], F32, name="dy0"), keep.tile([P, PACK, T], F32, name="dy1", tag="gate_runs")]
        for t in range(PACK - 1):
            nc.sync.dma_start(out=dy[0][:, t, :], in_=rows[0, t])
        for h in range(2):
            half = slice(h * T // 2, (h + 1) * T // 2)
            nc.sync.dma_start(out=dy[0][:, PACK - 1, half], in_=rows[0, PACK - 1][:, half])
        planes = [keep.tile([P, T], F32, name=f"plane{t}") for t in range(PACK)]
        for t in range(PACK):
            nc.sync.dma_start(out=planes[t][:], in_=rows[1, t])

        ww = keep.tile([P, (E + 1) * PASSES, 2 * K], U8, name="ww", align_bytes=64)
        nc.sync.dma_start(out=ww[:].bitcast(I32), in_=w_words.rearrange("e a p b -> p (e a) b").bitcast(I32))
        ws = keep.tile([P, (E + 1) * PASSES, K], U8, name="ws", align_bytes=64)
        nc.gpsimd.memset(ws[:].bitcast(I32), 0)
        for q in range(4):
            nc.sync.dma_start(
                out=ws[32 * q : 32 * q + 4].bitcast(I32),
                in_=w_scales[:, :, 4 * q : 4 * q + 4, :].rearrange("e a f k -> f (e a) k").bitcast(I32),
            )

        for c in range(CHUNKS):
            cols = slice(c * W, (c + 1) * W)
            nc.sync.dma_start(out=dy[1][:, :, cols], in_=rows[1].rearrange("t p n -> p t n")[:, :, cols])

        routed = [keep.tile([P, T], F32, name=f"routed{kb}") for kb in range(KB)]
        nc.vector.memset(routed[0][:], 0.0)
        nc.gpsimd.memset(routed[1][:], 0.0)

        def round_and_weave(dst, src, copy=nc.scalar.copy):
            copy(
                out=dst.rearrange("p (c i) t -> p c t i", i=LINE),
                in_=src.rearrange("p t (c i) -> p c t i", i=LINE),
            )

        def quantize(woven, name):
            width = woven.shape[1]
            codes = keep.tile([P, width], U32, name=name + "_codes", align_bytes=64)
            scales = keep.tile([P, width], U8, name=name + "_scales", align_bytes=64)
            nc.vector.quantize_mx(
                out=codes[:].bitcast(E5M2X4), scales=scales[:], in_=woven.rearrange("p c t -> p (c t)")
            )
            return [(codes[:, w : w + W], scales[:, w : w + W]) for w in range(0, width, W)]

        def product(acc, e, kb, operands):
            for a in range(PASSES):
                codes, scales = operands[a]
                nc.tensor.matmul_mx(
                    out=acc[:],
                    lhsT=ww[:, e * PASSES + a, 2 * P * kb : 2 * P * (kb + 1)].bitcast(E2M1X4),
                    lhsT_scale=ws[:, e * PASSES + a, P * kb : P * (kb + 1)],
                    rhs=codes.bitcast(E5M2X4),
                    rhs_scale=scales,
                    start=(a == 0),
                    stop=(a == PASSES - 1),
                )

        def expert_offsets(e):
            return offsets[:, e * C // PER_COLUMN : (e + 1) * C // PER_COLUMN]

        picked = keep.tile([P, PACK, S], F32, name="picked0", align_bytes=64)
        for t in range(PACK - 1):
            nc.vector.tensor_copy(picked[:, t, :], dy[0][:, t, :].indirect(offsets[:]))
        for e in range(E):
            nc.vector.tensor_copy(
                picked[:, PACK - 1, e * C : (e + 1) * C], dy[0][:, PACK - 1, :].indirect(expert_offsets(e))
            )

        g_first = keep.tile([P, S, PACK], BF16, name="g_first", align_bytes=64)
        for e in range(E):
            woven_words = g_first[:, e * C : (e + 1) * C, :].rearrange("p c t -> p (c t)").bitcast(F32)
            for h in range(2):
                back = psum.tile([P, 2, 2, P], F32, name="back", tag=f"bank{4 + h}")
                for i in range(2):
                    block = e * (C // P) + 2 * h + i
                    turned = psum.tile([P, PACK, P], F32, name="turned", tag=f"bank{block % 4}")
                    for t in reversed(range(PACK)):
                        nc.tensor.transpose(turned[:, t, :], picked[:, t, block * P : (block + 1) * P], ident[:])
                    pairs = keep.tile([P, 2, P, 2], BF16, name="pairs", tag=f"pairs{block % 4}", align_bytes=64)
                    nc.scalar.activation(
                        out=pairs[:],
                        in_=turned[:].rearrange("s (u j) p -> s u p j", j=2),
                        func=COPY,
                        scale=gate_cols[:, block : block + 1],
                    )
                    pair_words = pairs[:].rearrange("s u p j -> s (u p j)").bitcast(F32)
                    for u in range(2):
                        nc.tensor.transpose(back[:, i, u, :], pair_words[:, u * P : (u + 1) * P], ident[:])
                nc.scalar.copy(
                    out=woven_words[:, h * C : (h + 1) * C].rearrange("p (i s u) -> p i s u", i=2, u=2),
                    in_=back[:].rearrange("p i u s -> p i s u"),
                )

        gated = keep.tile([P, PACK, S], F32, name="gated", align_bytes=64)
        for t in range(PACK - 1):
            nc.vector.tensor_tensor(gated[:, t, :], planes[t][:].indirect(offsets[:]), gate_row[:], MULT)
        for e in range(E):
            slots = slice(e * C, (e + 1) * C)
            nc.vector.tensor_tensor(
                gated[:, PACK - 1, slots], planes[PACK - 1][:].indirect(expert_offsets(e)), gate_row[:, slots], MULT
            )
        g_mx = [[operand] for operand in quantize(g_first[:], "g_first")]

        for e, copy in enumerate((nc.scalar.copy, nc.vector.tensor_copy)):
            g_second = keep.tile([P, C, PACK], BF16, name="g_second", tag="pairs3", align_bytes=64)
            round_and_weave(g_second[:], gated[:, :, e * C : (e + 1) * C], copy)
            g_mx[e].extend(quantize(g_second[:], f"g_second{e}"))
            for kb in range(KB):
                acc = psum.tile([P, C], F32, name="acc", tag=f"bank{kb}")
                product(acc, e, kb, g_mx[e])
                dx = keep.tile([P, C], F32, name=f"dx{e}{kb}")
                nc.scalar.copy(out=dx[:], in_=acc[:])
                nc.vector.tensor_copy(routed[kb][:].indirect(expert_offsets(e)), dx[:])

        dy_mx = [[] for c in range(CHUNKS)]

        def shared_operands(woven, a, first):
            for j in range(0, woven.shape[1], PIECE):
                round_and_weave(woven[:, j : j + PIECE, :], dy[a][:, :, first * W + j : first * W + j + PIECE])
            for i, operand in enumerate(quantize(woven, f"dy{a}{first}")):
                dy_mx[first + i].insert(a, operand)

        early = keep.tile([P, EARLY * W, PACK], BF16, name="early", align_bytes=64)
        shared_operands(early[:], 0, 0)
        late = keep.tile([P, (PASSES * CHUNKS - EARLY) * W * PACK], BF16, name="late", tag="picked0", align_bytes=64)

        def rooms(first, count):
            return late[:, first * W * PACK : (first + count) * W * PACK]

        for a, first, count, room in ((1, 0, 1, 0), (0, EARLY, 2, CHUNKS), (1, 1, 1, 1), (1, 2, 2, 2)):
            shared_operands(rooms(room, count).rearrange("p (c t) -> p c t", t=PACK), a, first)

        for c in range(CHUNKS):
            result = rooms((c + 1) % CHUNKS, 1).bitcast(F32)
            for kb in range(KB):
                cols = slice(c * W, (c + 1) * W)
                acc = psum.tile([P, W], F32, name="ds", tag=f"bank{KB * c + kb}")
                product(acc, E, kb, dy_mx[c])
                nc.vector.tensor_tensor(result[:, kb * W : (kb + 1) * W], acc[:], routed[kb][:, cols], ADD)
                nc.sync.dma_start(out=out[kb * P : (kb + 1) * P, cols], in_=result[:, kb * W : (kb + 1) * W])
